import numpy as np
import ml_dtypes


def mxq(x, axis, fmt="e4m3"):
    dtype, down = {"e4m3": (ml_dtypes.float8_e4m3fn, 7), "e5m2": (ml_dtypes.float8_e5m2, 14)}[fmt]
    v = np.moveaxis(np.asarray(x, np.float32).astype(ml_dtypes.bfloat16).astype(np.float64), axis, -1)
    blocks = v.reshape(v.shape[:-1] + (-1, 32))
    amax = np.abs(blocks).max(-1, keepdims=True)
    byte = np.maximum(np.where(amax > 0, np.frexp(amax)[1] - 1 + 127, 0) - down, 1)
    scale = np.exp2(byte - 127.0)
    codes = (blocks / scale).astype(np.float32).astype(dtype).astype(np.float64)
    return np.moveaxis((codes * scale).reshape(v.shape), -1, axis)


WIDE = False


def mx_kscale(k):
    if not WIDE:
        return np.ones(k)
    levels = np.array([10, -10, 5, -5, 0])
    if k % 512:
        return np.exp2(np.random.permutation(np.resize(levels, k // 32))).repeat(32)
    a = np.empty((k // 512, 16))
    for p in range(k // 512):
        a[p, :8] = np.random.permutation(np.resize(levels, 8))
        for g in range(8):
            far = levels[np.abs(levels - a[p, g]) >= 10]
            a[p, g + 8] = far[np.random.randint(len(far))]
    return np.exp2(a.ravel()).repeat(32)


def f64(x):
    return np.asarray(x).astype(np.float64)


def striped(idx):
    return np.tile(idx.reshape(-1, 16).T, (8, 1)).astype(np.uint16)


def unstriped(offs):
    return offs[:16].T.reshape(-1).astype(np.int64)


E2M1 = np.array([0.0, 0.5, 1.0, 1.5, 2.0, 3.0, 4.0, 6.0, -0.0, -0.5, -1.0, -1.5, -2.0, -3.0, -4.0, -6.0])


def pack_weight(w, fmt):
    k, n = w.shape
    w = f64(np.asarray(w, np.float32).astype(ml_dtypes.bfloat16)).reshape(k // 32, 32, n)
    amax = np.abs(w).max(1)
    if fmt == "e4m3":
        byte = np.frexp(amax)[1] - 1 + 127 - 7
    else:
        mant, ex = np.frexp(amax / 6.0)
        byte = np.where(mant > 0.5, ex, ex - 1) + 127
    byte = np.clip(np.where(amax > 0, byte, 1), 1, 254)
    scaled = (w * np.exp2(127.0 - byte)[:, None, :]).reshape(k, n).astype(np.float32)
    by_word = np.ascontiguousarray(scaled.reshape(k // 512, 128, 4, n).transpose(0, 1, 3, 2))
    if fmt == "e4m3":
        words = by_word.astype(ml_dtypes.float8_e4m3fn).view(np.uint8)
    else:
        c = by_word.astype(ml_dtypes.float4_e2m1fn).view(np.uint8) & 0xF
        words = (c[..., 0::2] | (c[..., 1::2] << 4)).reshape(k // 512, 128, 2 * n)
    return np.ascontiguousarray(words), np.ascontiguousarray(byte.astype(np.uint8).reshape(k // 512, 16, n))


def unpack_weight(words, scales, fmt):
    g, _, n = scales.shape
    words = np.ascontiguousarray(words).reshape(g, 128, n, -1)
    if fmt == "e4m3":
        vals = words.view(ml_dtypes.float8_e4m3fn).astype(np.float64)
    else:
        nib = np.empty((g, 128, n, 4), np.uint8)
        nib[..., 0::2] = words & 0xF
        nib[..., 1::2] = words >> 4
        vals = E2M1[nib]
    vals = vals * np.repeat(np.exp2(scales.astype(np.float64) - 127.0), 8, axis=1)[..., None]
    return vals.transpose(0, 1, 3, 2).reshape(g * 512, n)


def gelu(v):
    return 0.5 * v * (1.0 + np.tanh(np.sqrt(2.0 / np.pi) * (v + 0.044715 * v**3)))


K, K2, H, N, T, TI, S, T2, P = 512, 1024, 1024, 512, 2048, 1024, 512, 2048, 1024

def setup_inputs():
    n = np.random.standard_normal
    s, s2, u = mx_kscale(K)[:, None], mx_kscale(K2)[:, None], mx_kscale(H)[:, None]
    d = {}
    d["tab_words"], d["tab_scales"] = pack_weight(n((K, T)) * s, "e4m3")
    d["tab2_words"], d["tab2_scales"] = pack_weight(n((K2, TI)) * s2, "e4m3")
    d["offs"] = striped(np.random.permutation(T)[:S])
    d["offs2"] = striped(np.random.permutation(TI)[:S])
    perm = np.random.permutation(T2)
    d["offs3"] = striped(perm[:S])
    d["offs4"] = striped(perm[S:2 * S])
    d["offs5"] = striped(np.random.permutation(T2)[:P])
    d["w1"] = (1.5 * n((K, H)) / K**0.5 / s).astype(np.float32)
    d["w2_words"], d["w2_scales"] = pack_weight(1.6 * n((K2, H)) / K2**0.5 / s2, "e2m1")
    d["g1"] = (np.exp(0.3 * n(H)) * u[:, 0]).astype(np.float32)
    d["g2"] = (1.4 * np.exp(0.3 * n(H)) * u[:, 0]).astype(np.float32)
    d["wg1"] = np.exp(0.3 * n((128, S))).astype(np.float32)
    d["wg2"] = np.exp(0.3 * n((128, S))).astype(np.float32)
    d["page0"] = (n((H, T2)) * u).astype(np.float32)
    d["wa_words"], d["wa_scales"] = pack_weight(n((H, N)) / H**0.5 / u, "e2m1")
    d["wb"] = (0.7 * n((H, N)) / H**0.5 / (u * u)).astype(np.float32)
    return d

def reference(tab_words, tab_scales, tab2_words, tab2_scales, offs, offs2, offs3, offs4, offs5,
              w1, w2_words, w2_scales, g1, g2, wg1, wg2, page0, wa_words, wa_scales, wb):
    v = unpack_weight(tab_words, tab_scales, "e4m3")[:, unstriped(offs)]
    v2 = unpack_weight(tab2_words, tab2_scales, "e4m3")[:, unstriped(offs2)]
    a = mxq(f64(w1), 0, "e4m3").T @ v
    h1 = np.log(1.0 + a * a) * f64(g1)[:, None]
    b = unpack_weight(w2_words, w2_scales, "e2m1").T @ v2
    h2 = np.tanh(b) * f64(g2)[:, None]
    page = f64(page0).copy()
    page[:, unstriped(offs3)] = np.tile(f64(wg1), (H // 128, 1)) * h1
    page[:, unstriped(offs4)] = np.tile(f64(wg2), (H // 128, 1)) * h2
    x = page[:, unstriped(offs5)]
    xb = mxq(x, 0, "e4m3")
    xx = mxq(x * x, 0, "e4m3")
    return unpack_weight(wa_words, wa_scales, "e2m1").T @ xb + mxq(f64(wb), 0, "e4m3").T @ xx

@@ -1,0 +1,324 @@
+from contextlib import ExitStack
+
+import concourse.mybir as mybir
+from concourse.masks import make_identity
+
+K, K2, H, N, T, TI, S, T2, P = 512, 1024, 1024, 512, 2048, 1024, 512, 2048, 1024
+FLOPS = 2 * (K * H * S + K2 * H * S + 2 * H * N * P)
+
+F32 = mybir.dt.float32
+BF16 = mybir.dt.bfloat16
+I32 = mybir.dt.int32
+U32 = mybir.dt.uint32
+U16 = mybir.dt.uint16
+U8 = mybir.dt.uint8
+FP8X4 = mybir.dt.float8_e4m3fn_x4
+FP4X4 = mybir.dt.float4_e2m1fn_x4
+ACT = mybir.ActivationFunctionType
+MULT = mybir.AluOpType.mult
+
+PARTS = 128
+PACK = 4
+K_PASS = PARTS * PACK
+H_PASSES = H // K_PASS
+K2_PASSES = K2 // K_PASS
+CHUNK = 256
+ALIGN = 64
+
+
+def tile_list_seal_archive_scores_kernel(
+    tc, tab_words, tab_scales, tab2_words, tab2_scales, offs, offs2, offs3, offs4, offs5,
+    w1, w2_words, w2_scales, g1, g2, wg1, wg2, page0, wa_words, wa_scales, wb, out,
+):
+    nc = tc.nc
+    with ExitStack() as ctx:
+        lists = ctx.enter_context(tc.tile_pool(name="lists", bufs=1))
+        sb = ctx.enter_context(tc.tile_pool(name="sb", bufs=1))
+        psum = ctx.enter_context(tc.psum_pool(name="psum", bufs=1))
+
+        def tile(name, shape, dtype, tag=None, bufs=1):
+            return sb.tile(shape, dtype, name=name, tag=tag or name, bufs=bufs, align_bytes=ALIGN)
+
+        def bank(name, tag, bufs):
+            return psum.tile([PARTS, 512], F32, name=name, tag=tag, bufs=bufs)
+
+        def load_list(name, src):
+            held = lists.tile([PARTS, src.shape[1]], U16, name=name)
+            nc.sync.dma_start(held[:], src)
+            return held
+
+        def scale_tile(name, src, engine):
+            held = tile(name, [PARTS, src.shape[0], src.shape[2]], U8)
+            engine.memset(held[:].bitcast(I32), 0)
+            return held
+
+        def load_scales(queue, held, src):
+            for q in range(4):
+                queue.dma_start(
+                    held[32 * q : 32 * q + 4].bitcast(I32),
+                    src[:, 4 * q : 4 * q + 4, :].rearrange("a r c -> r a c").bitcast(I32),
+                )
+
+        def load_table(name, src):
+            held = tile(name, [PARTS, src.shape[1]], I32)
+            nc.sync.dma_start(held[:], src.rearrange("p c i -> p (c i)").bitcast(I32))
+            return held
+
+        def load_fp4(name, src):
+            held = tile(name, [PARTS, src.shape[0], src.shape[2]], U8)
+            nc.sync.dma_start(held[:].bitcast(I32), src.rearrange("a p c -> p a c").bitcast(I32))
+            return held
+
+        def load_gain(name, src):
+            held = tile(name, [PARTS, H_PASSES, PACK], F32)
+            nc.sync.dma_start(held[:], src.rearrange("(b p t) -> p b t", p=PARTS, t=PACK))
+            return held
+
+        def load_wg(name, src, t0):
+            held = tile(name, [PARTS, 2, S], F32)
+            rows = src.rearrange("(m t) j -> m t j", t=PACK)[:, t0 : t0 + 2, :]
+            for q in range(4):
+                nc.sync.dma_start(held[32 * q : 32 * q + 32], rows)
+            return [held[:, 0, :], held[:, 1, :]]
+
+        def load_page(b, t):
+            held = tile("page%d%d" % (b, t), [PARTS, T2], F32, tag="page%d" % t)
+            rows = page0.rearrange("(b p t) c -> b t p c", p=PARTS, t=PACK)
+            nc.sync.dma_start(held[:], rows[b, t])
+            return held
+
+        def load_rows(name, src):
+            held = tile(name, [PARTS, PACK, 512], F32)
+            nc.sync.dma_start(held[:], src.rearrange("(p i) c -> p i c", i=PACK))
+            return held
+
+        def gather(name, dtype, window, offsets):
+            picked = tile(name, [PARTS, S], dtype)
+            nc.vector.tensor_copy(picked[:], window.indirect(offsets[:]))
+            return picked
+
+        def quantize(name, rounded, width, tag=None, bufs=1):
+            codes = tile(name + "_codes", [PARTS, width], U32, tag=tag and tag + "_codes", bufs=bufs)
+            scales = tile(name + "_scales", [PARTS, width], U8, tag=tag and tag + "_scales", bufs=bufs)
+            nc.vector.quantize_mx(out=codes[:].bitcast(FP8X4), scales=scales[:], in_=rounded[:])
+            return codes, scales
+
+        def interleave(name, planes, func, tag, bufs):
+            width = planes.shape[2]
+            rounded = tile(name, [PARTS, PACK * width], BF16, tag=tag, bufs=bufs)
+            nc.scalar.activation(
+                rounded[:].rearrange("p (c i t) -> p c t i", i=4, t=PACK),
+                planes[:].rearrange("p t (c i) -> p c t i", i=4),
+                func,
+            )
+            return rounded
+
+        tab2_s = scale_tile("tab2_s", tab2_scales, nc.gpsimd)
+        w2_s = scale_tile("w2_s", w2_scales, nc.vector)
+        tab_s = scale_tile("tab_s", tab_scales, nc.vector)
+        wa_s = scale_tile("wa_s", wa_scales, nc.vector)
+        ident = tile("ident", [PARTS, PARTS], F32)
+        make_identity(nc, ident[:])
+        idx2 = load_list("idx2", offs2)
+        idx4 = load_list("idx4", offs4)
+        gain2 = load_gain("gain2", g2)
+        tab2_w = [load_table("tab2_w0", tab2_words[0])]
+        load_scales(nc.sync, tab2_s, tab2_scales)
+        tab2_w.append(load_table("tab2_w1", tab2_words[1]))
+        w2_w = [load_fp4("w2_w0", w2_words[:, :, 0:1024])]
+        load_scales(nc.sync, w2_s, w2_scales)
+        tab_w = load_table("tab_w", tab_words[0])
+        idx1 = load_list("idx1", offs)
+        pages = {(0, 0): load_page(0, 0)}
+        load_scales(nc.sync, tab_s, tab_scales)
+        weight2 = load_wg("weight2a", wg2, 0)
+        w1_rows = [load_rows("w1_rows0", w1[:, 0:512])]
+        pages[0, 1] = load_page(0, 1)
+        weight2 = weight2 + load_wg("weight2b", wg2, 2)
+        pages[0, 2] = load_page(0, 2)
+        gain1 = load_gain("gain1", g1)
+        idx3 = load_list("idx3", offs3)
+        pages[0, 3] = load_page(0, 3)
+        weight1 = load_wg("weight1a", wg1, 0)
+        idx5 = load_list("idx5", offs5)
+        weight1 = weight1 + load_wg("weight1b", wg1, 2)
+        w1_rows.append(load_rows("w1_rows1", w1[:, 512:1024]))
+        w2_w.append(load_fp4("w2_w1", w2_words[:, :, 1024:2048]))
+        load_scales(nc.sync, wa_s, wa_scales)
+        wa_w = load_fp4("wa_w", wa_words)
+        wb_rows = [load_rows("wb_rows%d" % b, wb[K_PASS * b : K_PASS * (b + 1), :]) for b in range(H_PASSES)]
+
+        v2_s, v2_w = [], []
+        for a in range(K2_PASSES):
+            v2_s.append(gather("v2_s%d" % a, U8, tab2_s[:, a, :], idx2))
+            v2_w.append(gather("v2_w%d" % a, U32, tab2_w[a][:].bitcast(U32), idx2))
+        v_s = gather("v_s", U8, tab_s[:, 0, :], idx1)
+        v_w = gather("v_w", U32, tab_w[:].bitcast(U32), idx1)
+
+        h1, h2, logs, w1_q = {}, {}, {}, {}
+
+        def image_stream(b, groups):
+            blocks = range(S // PARTS)
+            accs = [bank("bT%d%d" % (b, jt), "wide", 4) for jt in blocks]
+            for a in range(K2_PASSES):
+                for jt in blocks:
+                    cols = slice(PARTS * jt, PARTS * (jt + 1))
+                    nc.tensor.matmul_mx(
+                        out=accs[jt][:],
+                        lhsT=v2_w[a][:, cols].bitcast(FP8X4),
+                        lhsT_scale=v2_s[a][:, cols],
+                        rhs=w2_w[b][:, a, :].bitcast(FP4X4),
+                        rhs_scale=w2_s[:, a, K_PASS * b : K_PASS * (b + 1)],
+                        start=(a == 0),
+                        stop=(a == K2_PASSES - 1),
+                    )
+            tanh = [tile("tanh%d%d" % (b, jt), [PARTS, PACK, PARTS], F32, tag="tanh", bufs=4) for jt in blocks]
+            for t0, t1 in groups:
+                for jt in blocks:
+                    by_slot = accs[jt][:].rearrange("p (m t) -> p t m", t=PACK)
+                    nc.scalar.activation(tanh[jt][:, t0:t1, :], by_slot[:, t0:t1, :], ACT.Tanh)
+                for t in range(t0, t1):
+                    turned = bank("turned%d%d" % (b, t), "turn", 2)
+                    for jt in blocks:
+                        nc.tensor.transpose(turned[:, PARTS * jt : PARTS * (jt + 1)], tanh[jt][:, t, :], ident[:])
+                    h2[b, t] = tile("h2_%d%d" % (b, t), [PARTS, S], F32, tag="h2", bufs=8)[:]
+                    nc.scalar.activation(h2[b, t], turned[:], ACT.Copy, scale=gain2[:, b, t : t + 1])
+
+        def round_w1(b):
+            rounded = tile("w1_bf%d" % b, [PARTS, PACK * 512], BF16, tag=("w1_bf0", "x0")[b])
+            nc.scalar.activation(
+                rounded[:].rearrange("p (t m i) -> p m i t", t=PACK, i=PACK),
+                w1_rows[b][:].rearrange("p i (m t) -> p m i t", t=PACK),
+                ACT.Copy,
+            )
+            w1_q[b] = quantize("w1_%d" % b, rounded, 512)
+
+        def spectral_stream(b, t):
+            codes, scales = w1_q[b]
+            cols = slice(PARTS * t, PARTS * (t + 1))
+            acc = bank("a%d%d" % (b, t), "lone", 2)
+            nc.tensor.matmul_mx(
+                out=acc[:], lhsT=codes[:, cols].bitcast(FP8X4), lhsT_scale=scales[:, cols],
+                rhs=v_w[:].bitcast(FP8X4), rhs_scale=v_s[:], start=True, stop=True,
+            )
+            h = tile("h1_%d%d" % (b, t), [PARTS, S], F32, tag="h1", bufs=8)
+            nc.scalar.activation(h[:], acc[:], ACT.Square)
+            nc.scalar.activation(h[:], h[:], ACT.Ln, bias=1.0)
+            logs[b, t] = h
+
+        def gain_spectral(b, t, dst):
+            nc.scalar.activation(dst, logs[b, t][:], ACT.Copy, scale=gain1[:, b, t : t + 1])
+            h1[b, t] = dst
+
+        def scatter(b, t, h, weight, offsets):
+            nc.vector.tensor_tensor(pages[b, t][:].indirect(offsets[:]), h[b, t], weight[t], MULT)
+
+        image_stream(0, [(0, 1), (1, PACK)])
+        round_w1(0)
+        for t in range(PACK):
+            scatter(0, t, h2, weight2, idx4)
+        for t in range(PACK):
+            spectral_stream(0, t)
+            gain_spectral(0, t, logs[0, t][:])
+        round_w1(1)
+        for t in range(PACK):
+            spectral_stream(1, t)
+        image_stream(1, [(0, PACK)])
+        wb_q = []
+        for b in range(H_PASSES):
+            wb_q.append(quantize("wb_%d" % b, interleave("wb_bf%d" % b, wb_rows[b], ACT.Copy, "tanh", 4), N))
+
+        x0 = tile("x0", [PARTS, PACK, P], F32, tag="x0")
+        scatter(0, 0, h1, weight1, idx3)
+        for t in range(PACK):
+            if t + 1 < PACK:
+                scatter(0, t + 1, h1, weight1, idx3)
+            nc.vector.tensor_copy(x0[:, t, :], pages[0, t][:].indirect(idx5[:]))
+        for t in range(PACK):
+            pages[1, t] = load_page(1, t)
+        x0_bf = interleave("x0_bf", x0, ACT.Copy, "wb_rows0", 1)
+        xx0_bf = interleave("xx0_bf", x0, ACT.Square, "wb_rows1", 1)
+        for t in range(PACK):
+            scatter(1, t, h2, weight2, idx4)
+        x0_q = quantize("x0", x0_bf, P)
+        xx0_q = quantize("xx0", xx0_bf, P)
+        h1_late = tile("h1_late", [PARTS, PACK, S], F32, tag="x0")
+        for t in range(PACK):
+            gain_spectral(1, t, h1_late[:, t, :])
+            scatter(1, t, h1, weight1, idx3)
+
+        def passes(acc, u, b, x_q, xx_q, base, first, last):
+            for half in range(2):
+                n0 = PARTS * (2 * u + half)
+                n_cols = slice(n0, n0 + PARTS)
+                for part in range(CHUNK // PARTS):
+                    lo = base + PARTS * part
+                    at = CHUNK * half + PARTS * part
+                    nc.tensor.matmul_mx(
+                        out=acc[:, at : at + PARTS],
+                        lhsT=wa_w[:, b, 2 * n0 : 2 * (n0 + PARTS)].bitcast(FP4X4),
+                        lhsT_scale=wa_s[:, b, n_cols],
+                        rhs=x_q[0][:, lo : lo + PARTS].bitcast(FP8X4),
+                        rhs_scale=x_q[1][:, lo : lo + PARTS],
+                        start=(first and half == 0 and part == 0),
+                        stop=False,
+                    )
+            for half in range(2):
+                n0 = PARTS * (2 * u + half)
+                n_cols = slice(n0, n0 + PARTS)
+                nc.tensor.matmul_mx(
+                    out=acc[:, CHUNK * half : CHUNK * (half + 1)],
+                    lhsT=wb_q[b][0][:, n_cols].bitcast(FP8X4),
+                    lhsT_scale=wb_q[b][1][:, n_cols],
+                    rhs=xx_q[0][:, base : base + CHUNK].bitcast(FP8X4),
+                    rhs_scale=xx_q[1][:, base : base + CHUNK],
+                    start=False,
+                    stop=(last and half == 1),
+                )
+
+        chunk_banks = [("wide", 4), ("wide", 4), ("turn", 2), ("lone", 2)]
+        chunks = P // CHUNK
+        picked = {}
+
+        def pick(c):
+            x1 = tile("x1_%d" % c, [PARTS, PACK, CHUNK], F32, tag="ring%d" % c)
+            for t in range(PACK):
+                entries = idx5[:, CHUNK // 16 * c : CHUNK // 16 * (c + 1)]
+                nc.vector.tensor_copy(x1[:, t, :], pages[1, t][:].indirect(entries))
+            if c == chunks - 1:
+                xx_bf = interleave("xx1_bf%d" % c, x1, ACT.Square, "ring%d" % (c + 2), 1)
+                x_bf = tile("x1_bf%d" % c, [PARTS, PACK * CHUNK], BF16, tag="tanh", bufs=4)
+                nc.vector.tensor_copy(
+                    x_bf[:].rearrange("p (c i t) -> p c t i", i=4, t=PACK),
+                    x1[:].rearrange("p t (c i) -> p c t i", i=4),
+                )
+            else:
+                x_bf = interleave("x1_bf%d" % c, x1, ACT.Copy, "tanh", 4)
+                xx_bf = interleave("xx1_bf%d" % c, x1, ACT.Square, "ring%d" % (c + 2), 1)
+            picked[c] = (x_bf, xx_bf)
+
+        def score(c):
+            x_q = quantize("x1_%d" % c, picked[c][0], CHUNK, tag="x1", bufs=4)
+            xx_q = quantize("xx1_%d" % c, picked[c][1], CHUNK, tag="x1", bufs=4)
+            accs = opened[c]
+            for u in range(2):
+                passes(accs[u], u, 1, x_q, xx_q, 0, False, True)
+                staged = tile("staged%d%d" % (c, u), [PARTS, 2, CHUNK], F32, tag="h2", bufs=8)
+                flat = staged[:].rearrange("p h j -> p (h j)")
+                if c == chunks - 1 and u == 1:
+                    nc.vector.tensor_copy(flat, accs[u][:])
+                else:
+                    nc.scalar.copy(flat, accs[u][:])
+                rows = out[2 * PARTS * u : 2 * PARTS * (u + 1), CHUNK * c : CHUNK * (c + 1)]
+                nc.sync.dma_start(rows.rearrange("(h p) j -> p h j", p=PARTS), staged[:])
+
+        opened = []
+        for c in range(chunks):
+            opened.append([bank("out%d%d" % (c, u), *chunk_banks[c]) for u in range(2)])
+            for u in range(2):
+                passes(opened[c][u], u, 0, x0_q, xx0_q, CHUNK * c, True, False)
+        pick(0)
+        for c in range(chunks):
+            if c + 1 < chunks:
+                pick(c + 1)
+            score(c)

@@ -23,7 +23,9 @@ K_PASS = PARTS * PACK
 H_PASSES = H // K_PASS
 K2_PASSES = K2 // K_PASS
 CHUNK = 256
+HALF = S // 2
 ALIGN = 64
+QUADRANTS = (0, 2, 1, 3)
 
 
 def tile_list_seal_archive_scores_kernel(
@@ -53,11 +55,16 @@ def tile_list_seal_archive_scores_kernel(
             return held
 
         def load_scales(queue, held, src):
-            for q in range(4):
+            for q in QUADRANTS:
                 queue.dma_start(
                     held[32 * q : 32 * q + 4].bitcast(I32),
                     src[:, 4 * q : 4 * q + 4, :].rearrange("a r c -> r a c").bitcast(I32),
                 )
+
+        def load_plane(name, src):
+            held = tile(name, [PARTS, src.shape[0], src.shape[2]], U8)
+            load_scales(nc.sync, held, src)
+            return held
 
         def load_table(name, src):
             held = tile(name, [PARTS, src.shape[1]], I32)
@@ -69,17 +76,17 @@ def tile_list_seal_archive_scores_kernel(
             nc.sync.dma_start(held[:].bitcast(I32), src.rearrange("a p c -> p a c").bitcast(I32))
             return held
 
-        def load_gain(name, src):
+        def load_gain(name, src, queue):
             held = tile(name, [PARTS, H_PASSES, PACK], F32)
-            nc.sync.dma_start(held[:], src.rearrange("(b p t) -> p b t", p=PARTS, t=PACK))
+            queue.dma_start(held[:], src.rearrange("(b p t) -> p b t", p=PARTS, t=PACK))
             return held
 
-        def load_wg(name, src, t0):
-            held = tile(name, [PARTS, 2, S], F32)
-            rows = src.rearrange("(m t) j -> m t j", t=PACK)[:, t0 : t0 + 2, :]
-            for q in range(4):
+        def load_wg(name, src, t0, t1):
+            held = tile(name, [PARTS, t1 - t0, S], F32)
+            rows = src.rearrange("(m t) j -> m t j", t=PACK)[:, t0:t1, :]
+            for q in QUADRANTS:
                 nc.sync.dma_start(held[32 * q : 32 * q + 32], rows)
-            return [held[:, 0, :], held[:, 1, :]]
+            return [held[:, t, :] for t in range(t1 - t0)]
 
         def load_page(b, t):
             held = tile("page%d%d" % (b, t), [PARTS, T2], F32, tag="page%d" % t)
@@ -93,8 +100,8 @@ def tile_list_seal_archive_scores_kernel(
             return held
 
         def gather(name, dtype, window, offsets):
-            picked = tile(name, [PARTS, S], dtype)
-            nc.vector.tensor_copy(picked[:], window.indirect(offsets[:]))
+            picked = tile(name, [PARTS, 16 * offsets.shape[1]], dtype)
+            nc.vector.tensor_copy(picked[:], window.indirect(offsets))
             return picked
 
         def quantize(name, rounded, width, tag=None, bufs=1):
@@ -114,75 +121,75 @@ def tile_list_seal_archive_scores_kernel(
             return rounded
 
         tab2_s = scale_tile("tab2_s", tab2_scales, nc.gpsimd)
-        w2_s = scale_tile("w2_s", w2_scales, nc.vector)
         tab_s = scale_tile("tab_s", tab_scales, nc.vector)
-        wa_s = scale_tile("wa_s", wa_scales, nc.vector)
         ident = tile("ident", [PARTS, PARTS], F32)
         make_identity(nc, ident[:])
         idx2 = load_list("idx2", offs2)
-        idx4 = load_list("idx4", offs4)
-        gain2 = load_gain("gain2", g2)
-        tab2_w = [load_table("tab2_w0", tab2_words[0])]
         load_scales(nc.sync, tab2_s, tab2_scales)
-        tab2_w.append(load_table("tab2_w1", tab2_words[1]))
+        tab2_w = [load_table("tab2_w%d" % a, tab2_words[a]) for a in range(K2_PASSES)]
         w2_w = [load_fp4("w2_w0", w2_words[:, :, 0:1024])]
-        load_scales(nc.sync, w2_s, w2_scales)
+        w2_s = [load_plane("w2_s0", w2_scales[:, :, 0:512])]
+        wg2_rows = tile("wg2_rows", [PARTS, S], F32, tag="ring2")
+        nc.sync.dma_start(wg2_rows[:], wg2)
         tab_w = load_table("tab_w", tab_words[0])
         idx1 = load_list("idx1", offs)
-        pages = {(0, 0): load_page(0, 0)}
+        idx4 = load_list("idx4", offs4)
+        gain2 = load_gain("gain2", g2, nc.gpsimd)
         load_scales(nc.sync, tab_s, tab_scales)
-        weight2 = load_wg("weight2a", wg2, 0)
-        w1_rows = [load_rows("w1_rows0", w1[:, 0:512])]
+        pages = {(0, 0): load_page(0, 0)}
         pages[0, 1] = load_page(0, 1)
-        weight2 = weight2 + load_wg("weight2b", wg2, 2)
+        w1_rows = [load_rows("w1_rows0", w1[:, 0:512])]
         pages[0, 2] = load_page(0, 2)
-        gain1 = load_gain("gain1", g1)
-        idx3 = load_list("idx3", offs3)
         pages[0, 3] = load_page(0, 3)
-        weight1 = load_wg("weight1a", wg1, 0)
+        gain1 = load_gain("gain1", g1, nc.sync)
+        idx3 = load_list("idx3", offs3)
+        weight1 = load_wg("weight1a", wg1, 0, 2)
         idx5 = load_list("idx5", offs5)
-        weight1 = weight1 + load_wg("weight1b", wg1, 2)
         w1_rows.append(load_rows("w1_rows1", w1[:, 512:1024]))
+        weight1 = weight1 + load_wg("weight1b", wg1, 2, 4)
         w2_w.append(load_fp4("w2_w1", w2_words[:, :, 1024:2048]))
-        load_scales(nc.sync, wa_s, wa_scales)
-        wa_w = load_fp4("wa_w", wa_words)
-        wb_rows = [load_rows("wb_rows%d" % b, wb[K_PASS * b : K_PASS * (b + 1), :]) for b in range(H_PASSES)]
+        w2_s.append(load_plane("w2_s1", w2_scales[:, :, 512:1024]))
 
         v2_s, v2_w = [], []
         for a in range(K2_PASSES):
-            v2_s.append(gather("v2_s%d" % a, U8, tab2_s[:, a, :], idx2))
-            v2_w.append(gather("v2_w%d" % a, U32, tab2_w[a][:].bitcast(U32), idx2))
-        v_s = gather("v_s", U8, tab_s[:, 0, :], idx1)
-        v_w = gather("v_w", U32, tab_w[:].bitcast(U32), idx1)
+            v2_s.append(gather("v2_s%d" % a, U8, tab2_s[:, a, :], idx2[:]))
+            v2_w.append(gather("v2_w%d" % a, U32, tab2_w[a][:].bitcast(U32), idx2[:]))
+        v_s = gather("v_s", U8, tab_s[:, 0, :], idx1[:])
+        v_w = gather("v_w", U32, tab_w[:].bitcast(U32), idx1[:])
 
-        h1, h2, logs, w1_q = {}, {}, {}, {}
+        h1, h2, logs, w1_q, w1_bf = {}, {}, {}, {}, {}
 
-        def image_stream(b, groups):
-            blocks = range(S // PARTS)
-            accs = [bank("bT%d%d" % (b, jt), "wide", 4) for jt in blocks]
+        blocks = range(S // PARTS)
+
+        def image_products(b, jts):
+            accs = {jt: bank("bT%d%d" % (b, jt), "wide", 4) for jt in jts}
             for a in range(K2_PASSES):
-                for jt in blocks:
-                    cols = slice(PARTS * jt, PARTS * (jt + 1))
+                for jt in jts:
                     nc.tensor.matmul_mx(
                         out=accs[jt][:],
-                        lhsT=v2_w[a][:, cols].bitcast(FP8X4),
-                        lhsT_scale=v2_s[a][:, cols],
+                        lhsT=v2_w[a][:, PARTS * jt : PARTS * (jt + 1)].bitcast(FP8X4),
+                        lhsT_scale=v2_s[a][:, PARTS * jt : PARTS * (jt + 1)],
                         rhs=w2_w[b][:, a, :].bitcast(FP4X4),
-                        rhs_scale=w2_s[:, a, K_PASS * b : K_PASS * (b + 1)],
+                        rhs_scale=w2_s[b][:, a, :],
                         start=(a == 0),
                         stop=(a == K2_PASSES - 1),
                     )
-            tanh = [tile("tanh%d%d" % (b, jt), [PARTS, PACK, PARTS], F32, tag="tanh", bufs=4) for jt in blocks]
-            for t0, t1 in groups:
-                for jt in blocks:
-                    by_slot = accs[jt][:].rearrange("p (m t) -> p t m", t=PACK)
-                    nc.scalar.activation(tanh[jt][:, t0:t1, :], by_slot[:, t0:t1, :], ACT.Tanh)
-                for t in range(t0, t1):
-                    turned = bank("turned%d%d" % (b, t), "turn", 2)
-                    for jt in blocks:
-                        nc.tensor.transpose(turned[:, PARTS * jt : PARTS * (jt + 1)], tanh[jt][:, t, :], ident[:])
-                    h2[b, t] = tile("h2_%d%d" % (b, t), [PARTS, S], F32, tag="h2", bufs=8)[:]
-                    nc.scalar.activation(h2[b, t], turned[:], ACT.Copy, scale=gain2[:, b, t : t + 1])
+            return accs
+
+        def image_tanh(acc, dst, t0, t1):
+            by_slot = acc[:].rearrange("p (m t) -> p t m", t=PACK)
+            nc.scalar.activation(dst, by_slot[:, t0:t1, :], ACT.Tanh)
+
+        def image_turn(b, t, tanh, jts):
+            turned = bank("turned%d%d%d" % (b, t, jts[0]), "turn", 2)
+            for jt in jts:
+                nc.tensor.transpose(turned[:, PARTS * jt : PARTS * (jt + 1)], tanh[jt], ident[:])
+            cols = slice(PARTS * jts[0], PARTS * (jts[-1] + 1))
+            nc.scalar.activation(h2[b, t][:, cols], turned[:, cols], ACT.Copy, scale=gain2[:, b, t : t + 1])
+
+        def image_tiles(b):
+            for t in range(PACK):
+                h2[b, t] = tile("h2_%d%d" % (b, t), [PARTS, S], F32, tag="h2", bufs=8)[:]
 
         def round_w1(b):
             rounded = tile("w1_bf%d" % b, [PARTS, PACK * 512], BF16, tag=("w1_bf0", "x0")[b])
@@ -191,6 +198,7 @@ def tile_list_seal_archive_scores_kernel(
                 w1_rows[b][:].rearrange("p i (m t) -> p m i t", t=PACK),
                 ACT.Copy,
             )
+            w1_bf[b] = rounded
             w1_q[b] = quantize("w1_%d" % b, rounded, 512)
 
         def spectral_stream(b, t):
@@ -201,7 +209,7 @@ def tile_list_seal_archive_scores_kernel(
                 out=acc[:], lhsT=codes[:, cols].bitcast(FP8X4), lhsT_scale=scales[:, cols],
                 rhs=v_w[:].bitcast(FP8X4), rhs_scale=v_s[:], start=True, stop=True,
             )
-            h = tile("h1_%d%d" % (b, t), [PARTS, S], F32, tag="h1", bufs=8)
+            h = tile("log%d%d" % (b, t), [PARTS, S], F32, *(("x0", 1) if (b, t) == (0, 1) else ("log", 5)))
             nc.scalar.activation(h[:], acc[:], ACT.Square)
             nc.scalar.activation(h[:], h[:], ACT.Ln, bias=1.0)
             logs[b, t] = h
@@ -213,17 +221,60 @@ def tile_list_seal_archive_scores_kernel(
         def scatter(b, t, h, weight, offsets):
             nc.vector.tensor_tensor(pages[b, t][:].indirect(offsets[:]), h[b, t], weight[t], MULT)
 
-        image_stream(0, [(0, 1), (1, PACK)])
+        wg2_turned = bank("wg2_turned", "lone", 2)
+        for jt in blocks:
+            cols = slice(PARTS * jt, PARTS * (jt + 1))
+            nc.tensor.transpose(wg2_turned[:, cols], wg2_rows[:, cols], ident[:])
+
+        def deal_wg2(t):
+            spread = tile("spread%d" % t, [PARTS, len(blocks), PARTS], F32, tag="ring%d" % (t % 2))
+            rows = wg2_turned[:].rearrange("p (j m t) -> p j m t", m=32, t=PACK)[:, :, :, t]
+            nc.scalar.copy(
+                spread[:].rearrange("p j (q m) -> p j q m", m=32),
+                rows.unsqueeze(2).to_broadcast([PARTS, len(blocks), 4, 32]),
+            )
+            dealt = bank("dealt%d" % t, "lone", 2)
+            for jt in blocks:
+                nc.tensor.transpose(dealt[:, PARTS * jt : PARTS * (jt + 1)], spread[:, jt, :], ident[:])
+            held = tile("weight2_%d" % t, [PARTS, S], F32)
+            nc.scalar.copy(held[:], dealt[:])
+            return held[:]
+
+        weight2 = [deal_wg2(0), deal_wg2(1)]
+        image_tiles(0)
+        accs = image_products(0, list(blocks))
+        first = tile("tanh_first", [PARTS, len(blocks), 1, PARTS], F32, tag="wb_rows1")
+        for jt in blocks:
+            image_tanh(accs[jt], first[:, jt], 0, 1)
+        image_turn(0, 0, [first[:, jt, 0, :] for jt in blocks], list(blocks))
+        rest = tile("tanh_rest", [PARTS, len(blocks), PACK - 1, PARTS], F32, tag="wb_rows1")
+        for jt in blocks:
+            image_tanh(accs[jt], rest[:, jt], 1, PACK)
+        for t in range(1, PACK):
+            image_turn(0, t, [rest[:, jt, t - 1, :] for jt in blocks], list(blocks))
+            if t + 1 < PACK:
+                weight2.append(deal_wg2(t + 1))
+        wb_rows = [load_rows("wb_rows%d" % b, wb[K_PASS * b : K_PASS * (b + 1), :]) for b in range(H_PASSES)]
+        wa_s = load_plane("wa_s", wa_scales)
+        wa_w = load_fp4("wa_w", wa_words)
         round_w1(0)
+        warm = tile("warm", [PARTS, 1], F32)
+        nc.scalar.activation(warm[:], w1_bf[0][:, 0:1], ACT.Ln, scale=0.0, bias=1.0)
         for t in range(PACK):
             scatter(0, t, h2, weight2, idx4)
         for t in range(PACK):
             spectral_stream(0, t)
-            gain_spectral(0, t, logs[0, t][:])
+            gain_spectral(0, t, tile("h1_0%d" % t, [PARTS, S], F32)[:])
         round_w1(1)
         for t in range(PACK):
             spectral_stream(1, t)
-        image_stream(1, [(0, PACK)])
+        image_tiles(1)
+        accs = image_products(1, list(blocks))
+        tanh = [tile("tanh1%d" % jt, [PARTS, PACK, PARTS], F32, tag="tanh", bufs=4) for jt in blocks]
+        for jt in blocks:
+            image_tanh(accs[jt], tanh[jt][:], 0, PACK)
+        for t in range(PACK):
+            image_turn(1, t, [tanh[jt][:, t, :] for jt in blocks], list(blocks))
         wb_q = []
         for b in range(H_PASSES):
             wb_q.append(quantize("wb_%d" % b, interleave("wb_bf%d" % b, wb_rows[b], ACT.Copy, "tanh", 4), N))
@@ -303,7 +354,12 @@ def tile_list_seal_archive_scores_kernel(
             accs = opened[c]
             for u in range(2):
                 passes(accs[u], u, 1, x_q, xx_q, 0, False, True)
-                staged = tile("staged%d%d" % (c, u), [PARTS, 2, CHUNK], F32, tag="h2", bufs=8)
+
+        def store(c):
+            accs = opened[c]
+            for u in range(2):
+                slot = ("ring3", 1) if (c, u) == (1, 1) else ("h2", 8)
+                staged = tile("staged%d%d" % (c, u), [PARTS, 2, CHUNK], F32, *slot)
                 flat = staged[:].rearrange("p h j -> p (h j)")
                 if c == chunks - 1 and u == 1:
                     nc.vector.tensor_copy(flat, accs[u][:])
@@ -318,7 +374,9 @@ def tile_list_seal_archive_scores_kernel(
             for u in range(2):
                 passes(opened[c][u], u, 0, x0_q, xx0_q, CHUNK * c, True, False)
         pick(0)
+        pick(1)
         for c in range(chunks):
-            if c + 1 < chunks:
-                pick(c + 1)
             score(c)
+            if c + 2 < chunks:
+                pick(c + 2)
+            store(c)

from contextlib import ExitStack

import concourse.mybir as mybir
from concourse.masks import make_identity

K, K2, H, N, T, TI, S, T2, P = 512, 1024, 1024, 512, 2048, 1024, 512, 2048, 1024
FLOPS = 2 * (K * H * S + K2 * H * S + 2 * H * N * P)

F32 = mybir.dt.float32
BF16 = mybir.dt.bfloat16
I32 = mybir.dt.int32
U32 = mybir.dt.uint32
U16 = mybir.dt.uint16
U8 = mybir.dt.uint8
FP8X4 = mybir.dt.float8_e4m3fn_x4
FP4X4 = mybir.dt.float4_e2m1fn_x4
ACT = mybir.ActivationFunctionType
MULT = mybir.AluOpType.mult

PARTS = 128
PACK = 4
K_PASS = PARTS * PACK
H_PASSES = H // K_PASS
K2_PASSES = K2 // K_PASS
CHUNK = 256
HALF = S // 2
ALIGN = 64
QUADRANTS = (0, 2, 1, 3)


def tile_list_seal_archive_scores_kernel(
    tc, tab_words, tab_scales, tab2_words, tab2_scales, offs, offs2, offs3, offs4, offs5,
    w1, w2_words, w2_scales, g1, g2, wg1, wg2, page0, wa_words, wa_scales, wb, out,
):
    nc = tc.nc
    with ExitStack() as ctx:
        lists = ctx.enter_context(tc.tile_pool(name="lists", bufs=1))
        sb = ctx.enter_context(tc.tile_pool(name="sb", bufs=1))
        psum = ctx.enter_context(tc.psum_pool(name="psum", bufs=1))

        def tile(name, shape, dtype, tag=None, bufs=1):
            return sb.tile(shape, dtype, name=name, tag=tag or name, bufs=bufs, align_bytes=ALIGN)

        def bank(name, tag, bufs):
            return psum.tile([PARTS, 512], F32, name=name, tag=tag, bufs=bufs)

        def load_list(name, src):
            held = lists.tile([PARTS, src.shape[1]], U16, name=name)
            nc.sync.dma_start(held[:], src)
            return held

        def scale_tile(name, src, engine):
            held = tile(name, [PARTS, src.shape[0], src.shape[2]], U8)
            engine.memset(held[:].bitcast(I32), 0)
            return held

        def load_scales(queue, held, src):
            for q in QUADRANTS:
                queue.dma_start(
                    held[32 * q : 32 * q + 4].bitcast(I32),
                    src[:, 4 * q : 4 * q + 4, :].rearrange("a r c -> r a c").bitcast(I32),
                )

        def load_plane(name, src):
            held = tile(name, [PARTS, src.shape[0], src.shape[2]], U8)
            load_scales(nc.sync, held, src)
            return held

        def load_table(name, src):
            held = tile(name, [PARTS, src.shape[1]], I32)
            nc.sync.dma_start(held[:], src.rearrange("p c i -> p (c i)").bitcast(I32))
            return held

        def load_fp4(name, src):
            held = tile(name, [PARTS, src.shape[0], src.shape[2]], U8)
            nc.sync.dma_start(held[:].bitcast(I32), src.rearrange("a p c -> p a c").bitcast(I32))
            return held

        def load_gain(name, src, queue):
            held = tile(name, [PARTS, H_PASSES, PACK], F32)
            queue.dma_start(held[:], src.rearrange("(b p t) -> p b t", p=PARTS, t=PACK))
            return held

        def load_wg(name, src, t0, t1):
            held = tile(name, [PARTS, t1 - t0, S], F32)
            rows = src.rearrange("(m t) j -> m t j", t=PACK)[:, t0:t1, :]
            for q in QUADRANTS:
                nc.sync.dma_start(held[32 * q : 32 * q + 32], rows)
            return [held[:, t, :] for t in range(t1 - t0)]

        def load_page(b, t):
            held = tile("page%d%d" % (b, t), [PARTS, T2], F32, tag="page%d" % t)
            rows = page0.rearrange("(b p t) c -> b t p c", p=PARTS, t=PACK)
            nc.sync.dma_start(held[:], rows[b, t])
            return held

        def load_rows(name, src):
            held = tile(name, [PARTS, PACK, 512], F32)
            nc.sync.dma_start(held[:], src.rearrange("(p i) c -> p i c", i=PACK))
            return held

        def gather(name, dtype, window, offsets):
            picked = tile(name, [PARTS, 16 * offsets.shape[1]], dtype)
            nc.vector.tensor_copy(picked[:], window.indirect(offsets))
            return picked

        def quantize(name, rounded, width, tag=None, bufs=1):
            codes = tile(name + "_codes", [PARTS, width], U32, tag=tag and tag + "_codes", bufs=bufs)
            scales = tile(name + "_scales", [PARTS, width], U8, tag=tag and tag + "_scales", bufs=bufs)
            nc.vector.quantize_mx(out=codes[:].bitcast(FP8X4), scales=scales[:], in_=rounded[:])
            return codes, scales

        def interleave(name, planes, func, tag, bufs):
            width = planes.shape[2]
            rounded = tile(name, [PARTS, PACK * width], BF16, tag=tag, bufs=bufs)
            nc.scalar.activation(
                rounded[:].rearrange("p (c i t) -> p c t i", i=4, t=PACK),
                planes[:].rearrange("p t (c i) -> p c t i", i=4),
                func,
            )
            return rounded

        tab2_s = scale_tile("tab2_s", tab2_scales, nc.gpsimd)
        tab_s = scale_tile("tab_s", tab_scales, nc.vector)
        ident = tile("ident", [PARTS, PARTS], F32)
        make_identity(nc, ident[:])
        idx2 = load_list("idx2", offs2)
        load_scales(nc.sync, tab2_s, tab2_scales)
        tab2_w = [load_table("tab2_w%d" % a, tab2_words[a]) for a in range(K2_PASSES)]
        w2_w = [load_fp4("w2_w0", w2_words[:, :, 0:1024])]
        w2_s = [load_plane("w2_s0", w2_scales[:, :, 0:512])]
        wg2_rows = tile("wg2_rows", [PARTS, S], F32, tag="ring2")
        nc.sync.dma_start(wg2_rows[:], wg2)
        tab_w = load_table("tab_w", tab_words[0])
        idx1 = load_list("idx1", offs)
        idx4 = load_list("idx4", offs4)
        gain2 = load_gain("gain2", g2, nc.gpsimd)
        load_scales(nc.sync, tab_s, tab_scales)
        pages = {(0, 0): load_page(0, 0)}
        pages[0, 1] = load_page(0, 1)
        w1_rows = [load_rows("w1_rows0", w1[:, 0:512])]
        pages[0, 2] = load_page(0, 2)
        pages[0, 3] = load_page(0, 3)
        gain1 = load_gain("gain1", g1, nc.sync)
        idx3 = load_list("idx3", offs3)
        weight1 = load_wg("weight1a", wg1, 0, 2)
        idx5 = load_list("idx5", offs5)
        w1_rows.append(load_rows("w1_rows1", w1[:, 512:1024]))
        weight1 = weight1 + load_wg("weight1b", wg1, 2, 4)
        w2_w.append(load_fp4("w2_w1", w2_words[:, :, 1024:2048]))
        w2_s.append(load_plane("w2_s1", w2_scales[:, :, 512:1024]))

        v2_s, v2_w = [], []
        for a in range(K2_PASSES):
            v2_s.append(gather("v2_s%d" % a, U8, tab2_s[:, a, :], idx2[:]))
            v2_w.append(gather("v2_w%d" % a, U32, tab2_w[a][:].bitcast(U32), idx2[:]))
        v_s = gather("v_s", U8, tab_s[:, 0, :], idx1[:])
        v_w = gather("v_w", U32, tab_w[:].bitcast(U32), idx1[:])

        h1, h2, logs, w1_q, w1_bf = {}, {}, {}, {}, {}

        blocks = range(S // PARTS)

        def image_products(b, jts):
            accs = {jt: bank("bT%d%d" % (b, jt), "wide", 4) for jt in jts}
            for a in range(K2_PASSES):
                for jt in jts:
                    nc.tensor.matmul_mx(
                        out=accs[jt][:],
                        lhsT=v2_w[a][:, PARTS * jt : PARTS * (jt + 1)].bitcast(FP8X4),
                        lhsT_scale=v2_s[a][:, PARTS * jt : PARTS * (jt + 1)],
                        rhs=w2_w[b][:, a, :].bitcast(FP4X4),
                        rhs_scale=w2_s[b][:, a, :],
                        start=(a == 0),
                        stop=(a == K2_PASSES - 1),
                    )
            return accs

        def image_tanh(acc, dst, t0, t1):
            by_slot = acc[:].rearrange("p (m t) -> p t m", t=PACK)
            nc.scalar.activation(dst, by_slot[:, t0:t1, :], ACT.Tanh)

        def image_turn(b, t, tanh, jts):
            turned = bank("turned%d%d%d" % (b, t, jts[0]), "turn", 2)
            for jt in jts:
                nc.tensor.transpose(turned[:, PARTS * jt : PARTS * (jt + 1)], tanh[jt], ident[:])
            cols = slice(PARTS * jts[0], PARTS * (jts[-1] + 1))
            nc.scalar.activation(h2[b, t][:, cols], turned[:, cols], ACT.Copy, scale=gain2[:, b, t : t + 1])

        def image_tiles(b):
            for t in range(PACK):
                h2[b, t] = tile("h2_%d%d" % (b, t), [PARTS, S], F32, tag="h2", bufs=8)[:]

        def round_w1(b):
            rounded = tile("w1_bf%d" % b, [PARTS, PACK * 512], BF16, tag=("w1_bf0", "x0")[b])
            nc.scalar.activation(
                rounded[:].rearrange("p (t m i) -> p m i t", t=PACK, i=PACK),
                w1_rows[b][:].rearrange("p i (m t) -> p m i t", t=PACK),
                ACT.Copy,
            )
            w1_bf[b] = rounded
            w1_q[b] = quantize("w1_%d" % b, rounded, 512)

        def spectral_stream(b, t):
            codes, scales = w1_q[b]
            cols = slice(PARTS * t, PARTS * (t + 1))
            acc = bank("a%d%d" % (b, t), "lone", 2)
            nc.tensor.matmul_mx(
                out=acc[:], lhsT=codes[:, cols].bitcast(FP8X4), lhsT_scale=scales[:, cols],
                rhs=v_w[:].bitcast(FP8X4), rhs_scale=v_s[:], start=True, stop=True,
            )
            h = tile("log%d%d" % (b, t), [PARTS, S], F32, *(("x0", 1) if (b, t) == (0, 1) else ("log", 5)))
            nc.scalar.activation(h[:], acc[:], ACT.Square)
            nc.scalar.activation(h[:], h[:], ACT.Ln, bias=1.0)
            logs[b, t] = h

        def gain_spectral(b, t, dst):
            nc.scalar.activation(dst, logs[b, t][:], ACT.Copy, scale=gain1[:, b, t : t + 1])
            h1[b, t] = dst

        def scatter(b, t, h, weight, offsets):
            nc.vector.tensor_tensor(pages[b, t][:].indirect(offsets[:]), h[b, t], weight[t], MULT)

        wg2_turned = bank("wg2_turned", "lone", 2)
        for jt in blocks:
            cols = slice(PARTS * jt, PARTS * (jt + 1))
            nc.tensor.transpose(wg2_turned[:, cols], wg2_rows[:, cols], ident[:])

        def deal_wg2(t):
            spread = tile("spread%d" % t, [PARTS, len(blocks), PARTS], F32, tag="ring%d" % (t % 2))
            rows = wg2_turned[:].rearrange("p (j m t) -> p j m t", m=32, t=PACK)[:, :, :, t]
            nc.scalar.copy(
                spread[:].rearrange("p j (q m) -> p j q m", m=32),
                rows.unsqueeze(2).to_broadcast([PARTS, len(blocks), 4, 32]),
            )
            dealt = bank("dealt%d" % t, "lone", 2)
            for jt in blocks:
                nc.tensor.transpose(dealt[:, PARTS * jt : PARTS * (jt + 1)], spread[:, jt, :], ident[:])
            held = tile("weight2_%d" % t, [PARTS, S], F32)
            nc.scalar.copy(held[:], dealt[:])
            return held[:]

        weight2 = [deal_wg2(0), deal_wg2(1)]
        image_tiles(0)
        accs = image_products(0, list(blocks))
        first = tile("tanh_first", [PARTS, len(blocks), 1, PARTS], F32, tag="wb_rows1")
        for jt in blocks:
            image_tanh(accs[jt], first[:, jt], 0, 1)
        image_turn(0, 0, [first[:, jt, 0, :] for jt in blocks], list(blocks))
        rest = tile("tanh_rest", [PARTS, len(blocks), PACK - 1, PARTS], F32, tag="wb_rows1")
        for jt in blocks:
            image_tanh(accs[jt], rest[:, jt], 1, PACK)
        for t in range(1, PACK):
            image_turn(0, t, [rest[:, jt, t - 1, :] for jt in blocks], list(blocks))
            if t + 1 < PACK:
                weight2.append(deal_wg2(t + 1))
        wb_rows = [load_rows("wb_rows%d" % b, wb[K_PASS * b : K_PASS * (b + 1), :]) for b in range(H_PASSES)]
        wa_s = load_plane("wa_s", wa_scales)
        wa_w = load_fp4("wa_w", wa_words)
        round_w1(0)
        warm = tile("warm", [PARTS, 1], F32)
        nc.scalar.activation(warm[:], w1_bf[0][:, 0:1], ACT.Ln, scale=0.0, bias=1.0)
        for t in range(PACK):
            scatter(0, t, h2, weight2, idx4)
        for t in range(PACK):
            spectral_stream(0, t)
            gain_spectral(0, t, tile("h1_0%d" % t, [PARTS, S], F32)[:])
        round_w1(1)
        for t in range(PACK):
            spectral_stream(1, t)
        image_tiles(1)
        accs = image_products(1, list(blocks))
        tanh = [tile("tanh1%d" % jt, [PARTS, PACK, PARTS], F32, tag="tanh", bufs=4) for jt in blocks]
        for jt in blocks:
            image_tanh(accs[jt], tanh[jt][:], 0, PACK)
        for t in range(PACK):
            image_turn(1, t, [tanh[jt][:, t, :] for jt in blocks], list(blocks))
        wb_q = []
        for b in range(H_PASSES):
            wb_q.append(quantize("wb_%d" % b, interleave("wb_bf%d" % b, wb_rows[b], ACT.Copy, "tanh", 4), N))

        x0 = tile("x0", [PARTS, PACK, P], F32, tag="x0")
        scatter(0, 0, h1, weight1, idx3)
        for t in range(PACK):
            if t + 1 < PACK:
                scatter(0, t + 1, h1, weight1, idx3)
            nc.vector.tensor_copy(x0[:, t, :], pages[0, t][:].indirect(idx5[:]))
        for t in range(PACK):
            pages[1, t] = load_page(1, t)
        x0_bf = interleave("x0_bf", x0, ACT.Copy, "wb_rows0", 1)
        xx0_bf = interleave("xx0_bf", x0, ACT.Square, "wb_rows1", 1)
        for t in range(PACK):
            scatter(1, t, h2, weight2, idx4)
        x0_q = quantize("x0", x0_bf, P)
        xx0_q = quantize("xx0", xx0_bf, P)
        h1_late = tile("h1_late", [PARTS, PACK, S], F32, tag="x0")
        for t in range(PACK):
            gain_spectral(1, t, h1_late[:, t, :])
            scatter(1, t, h1, weight1, idx3)

        def passes(acc, u, b, x_q, xx_q, base, first, last):
            for half in range(2):
                n0 = PARTS * (2 * u + half)
                n_cols = slice(n0, n0 + PARTS)
                for part in range(CHUNK // PARTS):
                    lo = base + PARTS * part
                    at = CHUNK * half + PARTS * part
                    nc.tensor.matmul_mx(
                        out=acc[:, at : at + PARTS],
                        lhsT=wa_w[:, b, 2 * n0 : 2 * (n0 + PARTS)].bitcast(FP4X4),
                        lhsT_scale=wa_s[:, b, n_cols],
                        rhs=x_q[0][:, lo : lo + PARTS].bitcast(FP8X4),
                        rhs_scale=x_q[1][:, lo : lo + PARTS],
                        start=(first and half == 0 and part == 0),
                        stop=False,
                    )
            for half in range(2):
                n0 = PARTS * (2 * u + half)
                n_cols = slice(n0, n0 + PARTS)
                nc.tensor.matmul_mx(
                    out=acc[:, CHUNK * half : CHUNK * (half + 1)],
                    lhsT=wb_q[b][0][:, n_cols].bitcast(FP8X4),
                    lhsT_scale=wb_q[b][1][:, n_cols],
                    rhs=xx_q[0][:, base : base + CHUNK].bitcast(FP8X4),
                    rhs_scale=xx_q[1][:, base : base + CHUNK],
                    start=False,
                    stop=(last and half == 1),
                )

        chunk_banks = [("wide", 4), ("wide", 4), ("turn", 2), ("lone", 2)]
        chunks = P // CHUNK
        picked = {}

        def pick(c):
            x1 = tile("x1_%d" % c, [PARTS, PACK, CHUNK], F32, tag="ring%d" % c)
            for t in range(PACK):
                entries = idx5[:, CHUNK // 16 * c : CHUNK // 16 * (c + 1)]
                nc.vector.tensor_copy(x1[:, t, :], pages[1, t][:].indirect(entries))
            if c == chunks - 1:
                xx_bf = interleave("xx1_bf%d" % c, x1, ACT.Square, "ring%d" % (c + 2), 1)
                x_bf = tile("x1_bf%d" % c, [PARTS, PACK * CHUNK], BF16, tag="tanh", bufs=4)
                nc.vector.tensor_copy(
                    x_bf[:].rearrange("p (c i t) -> p c t i", i=4, t=PACK),
                    x1[:].rearrange("p t (c i) -> p c t i", i=4),
                )
            else:
                x_bf = interleave("x1_bf%d" % c, x1, ACT.Copy, "tanh", 4)
                xx_bf = interleave("xx1_bf%d" % c, x1, ACT.Square, "ring%d" % (c + 2), 1)
            picked[c] = (x_bf, xx_bf)

        def score(c):
            x_q = quantize("x1_%d" % c, picked[c][0], CHUNK, tag="x1", bufs=4)
            xx_q = quantize("xx1_%d" % c, picked[c][1], CHUNK, tag="x1", bufs=4)
            accs = opened[c]
            for u in range(2):
                passes(accs[u], u, 1, x_q, xx_q, 0, False, True)

        def store(c):
            accs = opened[c]
            for u in range(2):
                slot = ("ring3", 1) if (c, u) == (1, 1) else ("h2", 8)
                staged = tile("staged%d%d" % (c, u), [PARTS, 2, CHUNK], F32, *slot)
                flat = staged[:].rearrange("p h j -> p (h j)")
                if c == chunks - 1 and u == 1:
                    nc.vector.tensor_copy(flat, accs[u][:])
                else:
                    nc.scalar.copy(flat, accs[u][:])
                rows = out[2 * PARTS * u : 2 * PARTS * (u + 1), CHUNK * c : CHUNK * (c + 1)]
                nc.sync.dma_start(rows.rearrange("(h p) j -> p h j", p=PARTS), staged[:])

        opened = []
        for c in range(chunks):
            opened.append([bank("out%d%d" % (c, u), *chunk_banks[c]) for u in range(2)])
            for u in range(2):
                passes(opened[c][u], u, 0, x0_q, xx0_q, CHUNK * c, True, False)
        pick(0)
        pick(1)
        for c in range(chunks):
            score(c)
            if c + 2 < chunks:
                pick(c + 2)
            store(c)
